import numpy as np
import ml_dtypes


def mxq(x, axis, fmt="e4m3"):
    dtype, down = {"e4m3": (ml_dtypes.float8_e4m3fn, 7), "e5m2": (ml_dtypes.float8_e5m2, 14)}[fmt]
    v = np.moveaxis(np.asarray(x, np.float32).astype(ml_dtypes.bfloat16).astype(np.float64), axis, -1)
    blocks = v.reshape(v.shape[:-1] + (-1, 32))
    amax = np.abs(blocks).max(-1, keepdims=True)
    byte = np.maximum(np.where(amax > 0, np.frexp(amax)[1] - 1 + 127, 0) - down, 1)
    scale = np.exp2(byte - 127.0)
    codes = (blocks / scale).astype(np.float32).astype(dtype).astype(np.float64)
    return np.moveaxis((codes * scale).reshape(v.shape), -1, axis)


WIDE = False


def mx_kscale(k):
    if not WIDE:
        return np.ones(k)
    levels = np.array([10, -10, 5, -5, 0])
    if k % 512:
        return np.exp2(np.random.permutation(np.resize(levels, k // 32))).repeat(32)
    a = np.empty((k // 512, 16))
    for p in range(k // 512):
        a[p, :8] = np.random.permutation(np.resize(levels, 8))
        for g in range(8):
            far = levels[np.abs(levels - a[p, g]) >= 10]
            a[p, g + 8] = far[np.random.randint(len(far))]
    return np.exp2(a.ravel()).repeat(32)


def f64(x):
    return np.asarray(x).astype(np.float64)


def striped(idx):
    return np.tile(np.asarray(idx).reshape(-1, 16).T, (8, 1)).astype(np.uint16)


def unstriped(offs):
    return offs[:16].T.reshape(-1).astype(np.int64)


E2M1 = np.array([0.0, 0.5, 1.0, 1.5, 2.0, 3.0, 4.0, 6.0, -0.0, -0.5, -1.0, -1.5, -2.0, -3.0, -4.0, -6.0])


def pack_weight(w, fmt):
    k, n = w.shape
    w = f64(np.asarray(w, np.float32).astype(ml_dtypes.bfloat16)).reshape(k // 32, 32, n)
    amax = np.abs(w).max(1)
    if fmt == "e4m3":
        byte = np.frexp(amax)[1] - 1 + 127 - 7
    else:
        mant, ex = np.frexp(amax / 6.0)
        byte = np.where(mant > 0.5, ex, ex - 1) + 127
    byte = np.clip(np.where(amax > 0, byte, 1), 1, 254)
    scaled = (w * np.exp2(127.0 - byte)[:, None, :]).reshape(k, n).astype(np.float32)
    by_word = np.ascontiguousarray(scaled.reshape(k // 512, 128, 4, n).transpose(0, 1, 3, 2))
    if fmt == "e4m3":
        words = by_word.astype(ml_dtypes.float8_e4m3fn).view(np.uint8)
    else:
        c = by_word.astype(ml_dtypes.float4_e2m1fn).view(np.uint8) & 0xF
        words = (c[..., 0::2] | (c[..., 1::2] << 4)).reshape(k // 512, 128, 2 * n)
    return np.ascontiguousarray(words), np.ascontiguousarray(byte.astype(np.uint8).reshape(k // 512, 16, n))


def unpack_weight(words, scales, fmt):
    g, _, n = scales.shape
    words = np.ascontiguousarray(words).reshape(g, 128, n, -1)
    if fmt == "e4m3":
        vals = words.view(ml_dtypes.float8_e4m3fn).astype(np.float64)
    else:
        nib = np.empty((g, 128, n, 4), np.uint8)
        nib[..., 0::2] = words & 0xF
        nib[..., 1::2] = words >> 4
        vals = E2M1[nib]
    vals = vals * np.repeat(np.exp2(scales.astype(np.float64) - 127.0), 8, axis=1)[..., None]
    return vals.transpose(0, 1, 3, 2).reshape(g * 512, n)


D, T, I, Q, J, U, G, M = 512, 2048, 512, 128, 512, 1024, 64, 512


def setup_inputs():
    n = np.random.standard_normal
    idx = np.random.permutation(T)[:I]
    idx2 = np.random.permutation(U)[:J]
    idx3 = np.random.permutation(M)[:G]
    fd = mx_kscale(D)
    fj = mx_kscale(J)
    tiesp = pack_weight(n((J, T)) * 0.08 / fj[:, None], "e4m3")
    return {
        "query": (n((D, Q)) * 0.65 / np.sqrt(D) * fd[:, None]).astype(np.float32),
        "hubs": (n((D, U)) / fd[:, None]).astype(np.float32),
        "hf": (np.random.uniform(0.5, 2.0, (J, 1)) * fj[:, None]).astype(np.float32),
        "ties_words": tiesp[0],
        "ties_scales": tiesp[1],
        "bar": (np.random.uniform(0.0, 0.8, (Q, 1))).astype(np.float32),
        "reserve": (np.random.uniform(20.0, 80.0, (Q, 1))).astype(np.float32),
        "worth": np.tile(np.random.uniform(0.2, 2.0, T), (128, 1)).astype(np.float32),
        "old": (1.0 * n((Q, M))).astype(np.float32),
        "offs": striped(idx),
        "offs2": striped(idx2),
        "offs3": striped(idx3),
    }


def reference(query, hubs, hf, ties_words, ties_scales, bar, reserve, worth, old, offs, offs2, offs3):
    idx = unstriped(offs)
    idx2 = unstriped(offs2)
    idx3 = unstriped(offs3)
    tiesu = unpack_weight(ties_words, ties_scales, "e4m3")
    hubsidx2q = mxq(f64(hubs)[:, idx2], 0, "e4m3")
    queryq = mxq(f64(query), 0, "e4m3")
    hb = hubsidx2q.T @ queryq
    hp = np.maximum(hb, 0.0) * f64(hf)
    hpq = mxq(hp, 0, "e4m3")
    tiesidxg = tiesu[:, idx]
    s = hpq.T @ tiesidxg
    ce = s - np.mean(s, axis=1, keepdims=True)
    sd = np.sqrt(np.mean(np.square(ce), axis=1, keepdims=True) + 0.1)
    p = np.square(np.maximum(ce / sd - f64(bar), 0.0))
    w = p / (np.sum(p, axis=1, keepdims=True) + f64(reserve))
    ws = w * f64(worth)[:1][:, idx] * 256.0
    wp = ws.reshape(Q, G, I // G).sum(axis=2)
    wf = np.zeros((Q, M))
    wf[:, idx3] = wp
    y = f64(old) + wf
    return y

@@ -1,0 +1,215 @@
+from contextlib import ExitStack
+
+import concourse.mybir as mybir
+from concourse.masks import make_identity
+
+F32 = mybir.dt.float32
+BF16 = mybir.dt.bfloat16
+I32 = mybir.dt.int32
+U32 = mybir.dt.uint32
+U16 = mybir.dt.uint16
+U8 = mybir.dt.uint8
+FP8X4 = mybir.dt.float8_e4m3fn_x4
+ALU = mybir.AluOpType
+ACT = mybir.ActivationFunctionType
+AXIS = mybir.AxisListType
+
+P = 128
+PACK = 4
+D, T, SLOTS, Q, J, U, G, M = 512, 2048, 512, 128, 512, 1024, 64, 512
+RUN = SLOTS // G
+HALF = SLOTS // 2
+LIST_COLS = SLOTS // 16
+J_VECTOR = 224
+WEAVE_VECTOR = 24
+
+FLOPS = 2 * D * J * Q + 2 * J * Q * SLOTS
+
+
+def tile_attend_relayed_outliers_pagesums_kernel(
+    tc, query, hubs, hf, ties_words, ties_scales, bar, reserve, worth, old, offs, offs2, offs3, out
+):
+    nc = tc.nc
+    with ExitStack() as ctx:
+        sb = ctx.enter_context(tc.tile_pool(name="sb", bufs=1))
+        ps = ctx.enter_context(tc.psum_pool(name="ps", bufs=1))
+
+        tok_list = sb.tile([P, LIST_COLS], U16, name="tok_list")
+        hub_list = sb.tile([P, LIST_COLS], U16, name="hub_list")
+        col_list = sb.tile([P, G // 16], U16, name="col_list")
+        tie_scales = sb.tile([P, T], U8, name="tie_scales", tag="hub_bf_then_old", align_bytes=64)
+        worth_row = sb.tile([P, T], F32, name="worth_row")
+        placed = sb.tile([P, M], F32, name="placed")
+        hf_sb = sb.tile([P, PACK], F32, name="hf_sb")
+        bar_sb = sb.tile([P, 1], F32, name="bar_sb")
+        reserve_sb = sb.tile([P, 1], F32, name="reserve_sb")
+        ident = sb.tile([P, P], F32, name="ident")
+        const256 = sb.tile([P, G], F32, name="const256")
+        q_raw = sb.tile([P, PACK, Q], F32, name="q_raw", tag="query_then_plane3")
+        planes = [
+            sb.tile([P, U], F32, name="plane0", tag="plane0_then_words"),
+            sb.tile([P, U], F32, name="plane1", tag="plane1_then_columns"),
+            sb.tile([P, U], F32, name="plane2"),
+        ]
+
+        nc.vector.memset(worth_row[:], 0.0)
+        nc.vector.memset(tie_scales[:].bitcast(I32), 0)
+        nc.vector.memset(placed[:], 0.0)
+        nc.vector.memset(const256[:], 256.0)
+
+        hub_planes = hubs.rearrange("(p t) u -> p t u", t=PACK)
+        nc.sync.dma_start(hub_list[:], offs2)
+        nc.sync.dma_start(tok_list[:], offs)
+        nc.sync.dma_start(col_list[:], offs3)
+        nc.scalar.dma_start(q_raw[:], query.rearrange("(p t) q -> p t q", t=PACK))
+        for t in range(PACK - 1):
+            nc.sync.dma_start(planes[t][:], hub_planes[:, t, :])
+        nc.scalar.dma_start(worth_row[0:1, :], worth[0:1, :])
+        for quad in range(4):
+            nc.scalar.dma_start(
+                tie_scales[32 * quad : 32 * quad + 4, :].bitcast(I32),
+                ties_scales[0, 4 * quad : 4 * quad + 4, :].bitcast(I32),
+            )
+        make_identity(nc, ident[:])
+        nc.gpsimd.dma_start(hf_sb[:], hf.rearrange("(p t) o -> p (t o)", t=PACK))
+        nc.gpsimd.dma_start(bar_sb[:], bar)
+        nc.gpsimd.dma_start(reserve_sb[:], reserve)
+
+        lo, hi = slice(0, LIST_COLS // 2), slice(LIST_COLS // 2, LIST_COLS)
+
+        q_bf = sb.tile([P, Q, PACK], BF16, name="q_bf", align_bytes=64)
+        nc.scalar.copy(q_bf[:], q_raw[:].rearrange("p t q -> p q t"))
+        planes.append(sb.tile([P, U], F32, name="plane3", tag="query_then_plane3"))
+        nc.sync.dma_start(planes[3][:], hub_planes[:, 3, :])
+        q_codes = sb.tile([P, Q], U32, name="q_codes", align_bytes=64)
+        q_scales = sb.tile([P, Q], U8, name="q_scales", align_bytes=64)
+
+        worth_g = sb.tile([P, SLOTS], F32, name="worth_g")
+        nc.vector.tensor_copy(worth_g[:], worth_row[:].indirect(tok_list[:]))
+        nc.vector.quantize_mx(out=q_codes[:].bitcast(FP8X4), scales=q_scales[:], in_=q_bf[:].rearrange("p q t -> p (q t)"))
+        turned = ps.tile([P, SLOTS // P, P], F32, name="turned")
+        for c in range(SLOTS // P):
+            nc.tensor.transpose(turned[:, c, :], worth_g[:, c * P : (c + 1) * P], ident[:])
+
+        scale_g = [sb.tile([P, HALF], U8, name="scale_g%d" % h, align_bytes=64) for h in range(2)]
+        for h, cols in enumerate((lo, hi)):
+            nc.vector.tensor_copy(scale_g[h][:], tie_scales[:].indirect(tok_list[:, cols]))
+        hub_bf = sb.tile([P, PACK, P, PACK], BF16, name="hub_bf", tag="hub_bf_then_old", align_bytes=64)
+        staged = sb.tile([P, PACK, J - J_VECTOR], BF16, name="staged", tag="staged_then_worth")
+
+        def gather_plane(t):
+            nc.scalar.activation(staged[:, t, :], planes[t][:].indirect(hub_list[:, J_VECTOR // 16 :]), ACT.Copy)
+            nc.vector.tensor_copy(
+                hub_bf[:, :, 0 : J_VECTOR // PACK, t].rearrange("p r m -> p m r"),
+                planes[t][:].indirect(hub_list[:, 0 : J_VECTOR // 16]),
+            )
+
+        gather_plane(0)
+        tie_words = sb.tile([P, T], U32, name="tie_words", tag="plane0_then_words")
+        nc.sync.dma_start(tie_words[:].bitcast(I32), ties_words[0].rearrange("p n t -> p (n t)").bitcast(I32))
+        gather_plane(1)
+        worth_cols = sb.tile([P, SLOTS // P], F32, name="worth_cols", tag="plane1_then_columns")
+        nc.vector.tensor_copy(worth_cols[:], turned[:, :, 0])
+        spread = ps.tile([P, SLOTS], F32, name="spread")
+        for c in range(SLOTS // P):
+            nc.tensor.transpose(spread[:, c * P : (c + 1) * P], worth_cols[:, c : c + 1].to_broadcast([P, P]), ident[:])
+        gather_plane(2)
+        gather_plane(3)
+
+        dealt = hub_bf[:, :, J_VECTOR // PACK : P, :].rearrange("p r (a b) t -> p a r b t", b=2)
+        listed = staged[:].rearrange("p t (a b r) -> p a r b t", b=2, r=PACK)
+        nc.vector.tensor_copy(dealt[:, 0:WEAVE_VECTOR], listed[:, 0:WEAVE_VECTOR])
+        nc.scalar.copy(dealt[:, WEAVE_VECTOR:], listed[:, WEAVE_VECTOR:])
+        worth_all = sb.tile([P, SLOTS], F32, name="worth_all", tag="staged_then_worth")
+        nc.scalar.copy(worth_all[:], spread[:])
+        neg_bar = sb.tile([P, 1], F32, name="neg_bar")
+        nc.scalar.activation(neg_bar[:], bar_sb[:], ACT.Copy, scale=-1.0)
+
+        hub_codes = sb.tile([P, J], U32, name="hub_codes", align_bytes=64)
+        hub_scales = sb.tile([P, J], U8, name="hub_scales", align_bytes=64)
+        hb = ps.tile([P, PACK, Q], F32, name="hb")
+        for r in range(PACK):
+            cols = slice(r * P, (r + 1) * P)
+            nc.vector.quantize_mx(
+                out=hub_codes[:, cols].bitcast(FP8X4),
+                scales=hub_scales[:, cols],
+                in_=hub_bf[:, r, :, :].rearrange("p m t -> p (m t)"),
+            )
+            nc.tensor.matmul_mx(
+                out=hb[:, r, :],
+                lhsT=hub_codes[:, cols].bitcast(FP8X4),
+                lhsT_scale=hub_scales[:, cols],
+                rhs=q_codes[:].bitcast(FP8X4),
+                rhs_scale=q_scales[:],
+                start=True,
+                stop=True,
+            )
+
+        old_sb = sb.tile([P, M], F32, name="old_sb", tag="hub_bf_then_old", align_bytes=64)
+        nc.sync.dma_start(old_sb[:], old)
+        hp_bf = sb.tile([P, Q, PACK], BF16, name="hp_bf", align_bytes=64)
+        nc.vector.scalar_tensor_tensor(
+            hp_bf[:],
+            hb[:].rearrange("p r q -> p q r"),
+            0.0,
+            hf_sb[:].unsqueeze(1).to_broadcast([P, Q, PACK]),
+            ALU.max,
+            ALU.mult,
+        )
+        word_g = [sb.tile([P, HALF], U32, name="word_g%d" % h, align_bytes=64) for h in range(2)]
+        nc.vector.tensor_copy(word_g[0][:], tie_words[:].indirect(tok_list[:, lo]))
+        hp_codes = sb.tile([P, Q], U32, name="hp_codes", align_bytes=64)
+        hp_scales = sb.tile([P, Q], U8, name="hp_scales", align_bytes=64)
+        nc.vector.quantize_mx(out=hp_codes[:].bitcast(FP8X4), scales=hp_scales[:], in_=hp_bf[:].rearrange("p q t -> p (q t)"))
+        nc.vector.tensor_copy(word_g[1][:], tie_words[:].indirect(tok_list[:, hi]))
+
+        score = [ps.tile([P, HALF], F32, name="score%d" % h) for h in range(2)]
+        stats = sb.tile([P, 12], F32, name="stats")
+        for h in range(2):
+            nc.tensor.matmul_mx(
+                out=score[h][:],
+                lhsT=hp_codes[:].bitcast(FP8X4),
+                lhsT_scale=hp_scales[:],
+                rhs=word_g[h][:].bitcast(FP8X4),
+                rhs_scale=scale_g[h][:],
+                start=True,
+                stop=True,
+            )
+            nc.vector.bn_stats(stats[:, 6 * h : 6 * h + 6], score[h][:])
+        mean_var = sb.tile([P, 2], F32, name="mean_var")
+        nc.vector.bn_aggr(mean_var[:], stats[:])
+        sd = sb.tile([P, 1], F32, name="sd")
+        nc.scalar.activation(sd[:], mean_var[:, 1:2], ACT.Sqrt, bias=0.1)
+        neg_mean = sb.tile([P, 1], F32, name="neg_mean")
+        nc.vector.tensor_scalar(neg_mean[:], mean_var[:, 0:1], -1.0, None, ALU.mult)
+        reserve_v = sb.tile([P, 1], F32, name="reserve_v")
+        nc.vector.tensor_scalar(reserve_v[:], mean_var[:, 1:2], 0.1, reserve_sb[:], ALU.add, ALU.mult)
+        neg_cut = sb.tile([P, 1], F32, name="neg_cut")
+        nc.scalar.activation(neg_cut[:], sd[:], ACT.Identity, bias=neg_mean[:], scale=neg_bar[:])
+
+        excess_w = sb.tile([P, SLOTS], F32, name="excess_w")
+        above = sb.tile([P, SLOTS], F32, name="above")
+        for h in range(2):
+            mine, other = slice(h * HALF, (h + 1) * HALF), slice((1 - h) * HALF, (2 - h) * HALF)
+            nc.vector.scalar_tensor_tensor(excess_w[:, mine], score[h][:], neg_cut[:], worth_all[:, mine], ALU.add, ALU.mult)
+            nc.scalar.activation(above[:, other], score[1 - h][:], ACT.Relu, bias=neg_cut[:])
+        squares = sb.tile([P, SLOTS], F32, name="squares")
+        part_sum = sb.tile([P, 1], F32, name="part_sum")
+        nc.scalar.activation(squares[:], above[:], ACT.Square, accum_out=part_sum[:])
+        denom = sb.tile([P, 1], F32, name="denom")
+        nc.scalar.activation(denom[:], part_sum[:], ACT.Identity, bias=reserve_v[:])
+        weighted = sb.tile([P, G, RUN], F32, name="weighted")
+        nc.vector.tensor_tensor(weighted[:].rearrange("p g k -> p (g k)"), excess_w[:], above[:], ALU.mult)
+        run_sums = sb.tile([P, G], F32, name="run_sums")
+        nc.vector.tensor_reduce(run_sums[:, 0 : G // 2], weighted[:, 0 : G // 2, :], AXIS.X, ALU.add)
+        inv = sb.tile([P, 1], F32, name="inv")
+        nc.vector.reciprocal(inv[:], denom[:])
+        nc.vector.tensor_reduce(run_sums[:, G // 2 : G], weighted[:, G // 2 : G, :], AXIS.X, ALU.add)
+        factor = sb.tile([P, G], F32, name="factor")
+        nc.scalar.activation(factor[:], const256[:], ACT.Copy, scale=inv[:])
+        nc.vector.tensor_tensor(placed[:].indirect(col_list[:]), run_sums[:], factor[:], ALU.mult)
+        for h, queue in enumerate((nc.sync, nc.scalar)):
+            cols = slice(h * (M // 2), (h + 1) * (M // 2))
+            result = sb.tile([P, M // 2], F32, name="result%d" % h)
+            nc.vector.tensor_tensor(result[:], placed[:, cols], old_sb[:, cols], ALU.add)
+            queue.dma_start(out[:, cols], result[:])

@@ -1,7 +1,6 @@
 from contextlib import ExitStack
 
 import concourse.mybir as mybir
-from concourse.masks import make_identity
 
 F32 = mybir.dt.float32
 BF16 = mybir.dt.bfloat16
@@ -19,9 +18,9 @@ PACK = 4
 D, T, SLOTS, Q, J, U, G, M = 512, 2048, 512, 128, 512, 1024, 64, 512
 RUN = SLOTS // G
 HALF = SLOTS // 2
+QUARTER = SLOTS // 4
 LIST_COLS = SLOTS // 16
 J_VECTOR = 224
-WEAVE_VECTOR = 24
 
 FLOPS = 2 * D * J * Q + 2 * J * Q * SLOTS
 
@@ -37,97 +36,72 @@ def tile_attend_relayed_outliers_pagesums_kernel(
         tok_list = sb.tile([P, LIST_COLS], U16, name="tok_list")
         hub_list = sb.tile([P, LIST_COLS], U16, name="hub_list")
         col_list = sb.tile([P, G // 16], U16, name="col_list")
-        tie_scales = sb.tile([P, T], U8, name="tie_scales", tag="hub_bf_then_old", align_bytes=64)
-        worth_row = sb.tile([P, T], F32, name="worth_row")
+        planes = [sb.tile([P, U], F32, name="plane%d" % t) for t in range(PACK)]
+        tie_words = sb.tile([P, T], U32, name="tie_words")
+        tie_scales = sb.tile([P, T], U8, name="tie_scales")
+        worth_sb = sb.tile([P, T], F32, name="worth_sb", tag="worth_then_sd")
+        q_raw = sb.tile([P, PACK, Q], F32, name="q_raw")
+        old_sb = sb.tile([P, M], F32, name="old_sb")
         placed = sb.tile([P, M], F32, name="placed")
-        hf_sb = sb.tile([P, PACK], F32, name="hf_sb")
-        bar_sb = sb.tile([P, 1], F32, name="bar_sb")
+        hf_sb = sb.tile([P, PACK], F32, name="hf_sb", tag="hf_then_words", align_bytes=64)
+        row_stats = sb.tile([P, 16], F32, name="row_stats")
         reserve_sb = sb.tile([P, 1], F32, name="reserve_sb")
-        ident = sb.tile([P, P], F32, name="ident")
         const256 = sb.tile([P, G], F32, name="const256")
-        q_raw = sb.tile([P, PACK, Q], F32, name="q_raw", tag="query_then_plane3")
-        planes = [
-            sb.tile([P, U], F32, name="plane0", tag="plane0_then_words"),
-            sb.tile([P, U], F32, name="plane1", tag="plane1_then_columns"),
-            sb.tile([P, U], F32, name="plane2"),
-        ]
 
-        nc.vector.memset(worth_row[:], 0.0)
         nc.vector.memset(tie_scales[:].bitcast(I32), 0)
         nc.vector.memset(placed[:], 0.0)
-        nc.vector.memset(const256[:], 256.0)
+        nc.scalar.activation(const256[:], placed[:, 0:G], ACT.Sqrt, bias=65536.0)
 
         hub_planes = hubs.rearrange("(p t) u -> p t u", t=PACK)
         nc.sync.dma_start(hub_list[:], offs2)
         nc.sync.dma_start(tok_list[:], offs)
-        nc.sync.dma_start(col_list[:], offs3)
-        nc.scalar.dma_start(q_raw[:], query.rearrange("(p t) q -> p t q", t=PACK))
-        for t in range(PACK - 1):
-            nc.sync.dma_start(planes[t][:], hub_planes[:, t, :])
-        nc.scalar.dma_start(worth_row[0:1, :], worth[0:1, :])
+        nc.sync.dma_start(planes[0][:], hub_planes[:, 0, :])
         for quad in range(4):
-            nc.scalar.dma_start(
+            nc.sync.dma_start(
                 tie_scales[32 * quad : 32 * quad + 4, :].bitcast(I32),
                 ties_scales[0, 4 * quad : 4 * quad + 4, :].bitcast(I32),
             )
-        make_identity(nc, ident[:])
-        nc.gpsimd.dma_start(hf_sb[:], hf.rearrange("(p t) o -> p (t o)", t=PACK))
-        nc.gpsimd.dma_start(bar_sb[:], bar)
-        nc.gpsimd.dma_start(reserve_sb[:], reserve)
+        for t in range(1, PACK):
+            nc.sync.dma_start(planes[t][:], hub_planes[:, t, :])
+        nc.sync.dma_start(q_raw[:], query.rearrange("(p t) q -> p t q", t=PACK))
+        nc.sync.dma_start(tie_words[:].bitcast(I32), ties_words[0].rearrange("p n t -> p (n t)").bitcast(I32))
+        nc.sync.dma_start(hf_sb[:], hf.rearrange("(p t) o -> p (t o)", t=PACK))
+        nc.sync.dma_start(worth_sb[:], worth)
+        nc.sync.dma_start(row_stats[:, 8:9], bar)
+        nc.sync.dma_start(reserve_sb[:], reserve)
+        nc.sync.dma_start(col_list[:], offs3)
+        nc.sync.dma_start(old_sb[:], old)
 
         lo, hi = slice(0, LIST_COLS // 2), slice(LIST_COLS // 2, LIST_COLS)
 
-        q_bf = sb.tile([P, Q, PACK], BF16, name="q_bf", align_bytes=64)
-        nc.scalar.copy(q_bf[:], q_raw[:].rearrange("p t q -> p q t"))
-        planes.append(sb.tile([P, U], F32, name="plane3", tag="query_then_plane3"))
-        nc.sync.dma_start(planes[3][:], hub_planes[:, 3, :])
-        q_codes = sb.tile([P, Q], U32, name="q_codes", align_bytes=64)
-        q_scales = sb.tile([P, Q], U8, name="q_scales", align_bytes=64)
-
-        worth_g = sb.tile([P, SLOTS], F32, name="worth_g")
-        nc.vector.tensor_copy(worth_g[:], worth_row[:].indirect(tok_list[:]))
-        nc.vector.quantize_mx(out=q_codes[:].bitcast(FP8X4), scales=q_scales[:], in_=q_bf[:].rearrange("p q t -> p (q t)"))
-        turned = ps.tile([P, SLOTS // P, P], F32, name="turned")
-        for c in range(SLOTS // P):
-            nc.tensor.transpose(turned[:, c, :], worth_g[:, c * P : (c + 1) * P], ident[:])
-
+        hub_bf = sb.tile([P, PACK, P, PACK], BF16, name="hub_bf", align_bytes=64)
+        staged = sb.tile([P, PACK, J - J_VECTOR], BF16, name="staged")
         scale_g = [sb.tile([P, HALF], U8, name="scale_g%d" % h, align_bytes=64) for h in range(2)]
-        for h, cols in enumerate((lo, hi)):
-            nc.vector.tensor_copy(scale_g[h][:], tie_scales[:].indirect(tok_list[:, cols]))
-        hub_bf = sb.tile([P, PACK, P, PACK], BF16, name="hub_bf", tag="hub_bf_then_old", align_bytes=64)
-        staged = sb.tile([P, PACK, J - J_VECTOR], BF16, name="staged", tag="staged_then_worth")
-
-        def gather_plane(t):
+        for t in range(PACK):
             nc.scalar.activation(staged[:, t, :], planes[t][:].indirect(hub_list[:, J_VECTOR // 16 :]), ACT.Copy)
             nc.vector.tensor_copy(
                 hub_bf[:, :, 0 : J_VECTOR // PACK, t].rearrange("p r m -> p m r"),
                 planes[t][:].indirect(hub_list[:, 0 : J_VECTOR // 16]),
             )
+            if t in (0, 1):
+                nc.vector.tensor_copy(scale_g[t][:], tie_scales[:].indirect(tok_list[:, (lo, hi)[t]]))
+        nc.vector.tensor_copy(
+            hub_bf[:, :, J_VECTOR // PACK : P, :].rearrange("p r (a b) t -> p a r b t", b=2),
+            staged[:].rearrange("p t (a b r) -> p a r b t", b=2, r=PACK),
+        )
 
-        gather_plane(0)
-        tie_words = sb.tile([P, T], U32, name="tie_words", tag="plane0_then_words")
-        nc.sync.dma_start(tie_words[:].bitcast(I32), ties_words[0].rearrange("p n t -> p (n t)").bitcast(I32))
-        gather_plane(1)
-        worth_cols = sb.tile([P, SLOTS // P], F32, name="worth_cols", tag="plane1_then_columns")
-        nc.vector.tensor_copy(worth_cols[:], turned[:, :, 0])
-        spread = ps.tile([P, SLOTS], F32, name="spread")
-        for c in range(SLOTS // P):
-            nc.tensor.transpose(spread[:, c * P : (c + 1) * P], worth_cols[:, c : c + 1].to_broadcast([P, P]), ident[:])
-        gather_plane(2)
-        gather_plane(3)
+        q_bf = sb.tile([P, Q, PACK], BF16, name="q_bf", align_bytes=64)
+        nc.scalar.copy(q_bf[:], q_raw[:].rearrange("p t q -> p q t"))
 
-        dealt = hub_bf[:, :, J_VECTOR // PACK : P, :].rearrange("p r (a b) t -> p a r b t", b=2)
-        listed = staged[:].rearrange("p t (a b r) -> p a r b t", b=2, r=PACK)
-        nc.vector.tensor_copy(dealt[:, 0:WEAVE_VECTOR], listed[:, 0:WEAVE_VECTOR])
-        nc.scalar.copy(dealt[:, WEAVE_VECTOR:], listed[:, WEAVE_VECTOR:])
-        worth_all = sb.tile([P, SLOTS], F32, name="worth_all", tag="staged_then_worth")
-        nc.scalar.copy(worth_all[:], spread[:])
-        neg_bar = sb.tile([P, 1], F32, name="neg_bar")
-        nc.scalar.activation(neg_bar[:], bar_sb[:], ACT.Copy, scale=-1.0)
+        worth_all = sb.tile([P, SLOTS], F32, name="worth_all")
+        nc.scalar.activation(worth_all[:], worth_sb[:].indirect(tok_list[:]), ACT.Copy)
 
         hub_codes = sb.tile([P, J], U32, name="hub_codes", align_bytes=64)
         hub_scales = sb.tile([P, J], U8, name="hub_scales", align_bytes=64)
+        q_codes = sb.tile([P, Q], U32, name="q_codes", align_bytes=64)
+        q_scales = sb.tile([P, Q], U8, name="q_scales", align_bytes=64)
         hb = ps.tile([P, PACK, Q], F32, name="hb")
+        nc.vector.quantize_mx(out=q_codes[:].bitcast(FP8X4), scales=q_scales[:], in_=q_bf[:].rearrange("p q t -> p (q t)"))
         for r in range(PACK):
             cols = slice(r * P, (r + 1) * P)
             nc.vector.quantize_mx(
@@ -145,9 +119,7 @@ def tile_attend_relayed_outliers_pagesums_kernel(
                 stop=True,
             )
 
-        old_sb = sb.tile([P, M], F32, name="old_sb", tag="hub_bf_then_old", align_bytes=64)
-        nc.sync.dma_start(old_sb[:], old)
-        hp_bf = sb.tile([P, Q, PACK], BF16, name="hp_bf", align_bytes=64)
+        hp_bf = sb.tile([P, Q, PACK], BF16, name="hp_bf", tag="hp_then_words", align_bytes=64)
         nc.vector.scalar_tensor_tensor(
             hp_bf[:],
             hb[:].rearrange("p r q -> p q r"),
@@ -156,55 +128,66 @@ def tile_attend_relayed_outliers_pagesums_kernel(
             ALU.max,
             ALU.mult,
         )
-        word_g = [sb.tile([P, HALF], U32, name="word_g%d" % h, align_bytes=64) for h in range(2)]
-        nc.vector.tensor_copy(word_g[0][:], tie_words[:].indirect(tok_list[:, lo]))
+        score = [ps.tile([P, HALF], F32, name="score%d" % h) for h in range(2)]
         hp_codes = sb.tile([P, Q], U32, name="hp_codes", align_bytes=64)
         hp_scales = sb.tile([P, Q], U8, name="hp_scales", align_bytes=64)
-        nc.vector.quantize_mx(out=hp_codes[:].bitcast(FP8X4), scales=hp_scales[:], in_=hp_bf[:].rearrange("p q t -> p (q t)"))
-        nc.vector.tensor_copy(word_g[1][:], tie_words[:].indirect(tok_list[:, hi]))
 
-        score = [ps.tile([P, HALF], F32, name="score%d" % h) for h in range(2)]
-        stats = sb.tile([P, 12], F32, name="stats")
-        for h in range(2):
+        def gather_words(first, count, tag):
+            words = sb.tile([P, count], U32, name=tag + "_words", tag=tag, align_bytes=64)
+            nc.vector.tensor_copy(words[:], tie_words[:].indirect(tok_list[:, first // 16 : (first + count) // 16]))
+            return words
+
+        def score_slots(first, count, words):
+            h, cols = first // HALF, slice(first % HALF, first % HALF + count)
             nc.tensor.matmul_mx(
-                out=score[h][:],
+                out=score[h][:, cols],
                 lhsT=hp_codes[:].bitcast(FP8X4),
                 lhsT_scale=hp_scales[:],
-                rhs=word_g[h][:].bitcast(FP8X4),
-                rhs_scale=scale_g[h][:],
+                rhs=words[:].bitcast(FP8X4),
+                rhs_scale=scale_g[h][:, cols],
                 start=True,
                 stop=True,
             )
-            nc.vector.bn_stats(stats[:, 6 * h : 6 * h + 6], score[h][:])
-        mean_var = sb.tile([P, 2], F32, name="mean_var")
-        nc.vector.bn_aggr(mean_var[:], stats[:])
-        sd = sb.tile([P, 1], F32, name="sd")
-        nc.scalar.activation(sd[:], mean_var[:, 1:2], ACT.Sqrt, bias=0.1)
-        neg_mean = sb.tile([P, 1], F32, name="neg_mean")
-        nc.vector.tensor_scalar(neg_mean[:], mean_var[:, 0:1], -1.0, None, ALU.mult)
-        reserve_v = sb.tile([P, 1], F32, name="reserve_v")
-        nc.vector.tensor_scalar(reserve_v[:], mean_var[:, 1:2], 0.1, reserve_sb[:], ALU.add, ALU.mult)
-        neg_cut = sb.tile([P, 1], F32, name="neg_cut")
-        nc.scalar.activation(neg_cut[:], sd[:], ACT.Identity, bias=neg_mean[:], scale=neg_bar[:])
 
-        excess_w = sb.tile([P, SLOTS], F32, name="excess_w")
-        above = sb.tile([P, SLOTS], F32, name="above")
+        words_a = gather_words(0, HALF, "first_half")
+        words_b = gather_words(HALF, QUARTER, "hf_then_words")
+        nc.vector.quantize_mx(out=hp_codes[:].bitcast(FP8X4), scales=hp_scales[:], in_=hp_bf[:].rearrange("p q t -> p (q t)"))
+        words_c = gather_words(HALF + QUARTER, QUARTER, "hp_then_words")
+        score_slots(0, HALF, words_a)
+        score_slots(HALF, QUARTER, words_b)
+        score_slots(HALF + QUARTER, QUARTER, words_c)
+        stats = sb.tile([P, 12], F32, name="stats")
         for h in range(2):
-            mine, other = slice(h * HALF, (h + 1) * HALF), slice((1 - h) * HALF, (2 - h) * HALF)
-            nc.vector.scalar_tensor_tensor(excess_w[:, mine], score[h][:], neg_cut[:], worth_all[:, mine], ALU.add, ALU.mult)
-            nc.scalar.activation(above[:, other], score[1 - h][:], ACT.Relu, bias=neg_cut[:])
-        squares = sb.tile([P, SLOTS], F32, name="squares")
-        part_sum = sb.tile([P, 1], F32, name="part_sum")
-        nc.scalar.activation(squares[:], above[:], ACT.Square, accum_out=part_sum[:])
-        denom = sb.tile([P, 1], F32, name="denom")
-        nc.scalar.activation(denom[:], part_sum[:], ACT.Identity, bias=reserve_v[:])
-        weighted = sb.tile([P, G, RUN], F32, name="weighted")
-        nc.vector.tensor_tensor(weighted[:].rearrange("p g k -> p (g k)"), excess_w[:], above[:], ALU.mult)
+            nc.vector.bn_stats(stats[:, 6 * h : 6 * h + 6], score[h][:])
+        nc.vector.bn_aggr(row_stats[:, 0:2], stats[:])
+        sd = sb.tile([P, 1], F32, name="sd", tag="worth_then_sd")
+        nc.scalar.activation(sd[:], row_stats[:, 1:2], ACT.Sqrt, bias=0.1)
+        negated = sb.tile([P, 2], F32, name="negated")
+        nc.vector.tensor_scalar(negated[:], row_stats[:, 0:9:8], -1.0, None, ALU.mult)
+        reserve_v = sb.tile([P, 1], F32, name="reserve_v")
+        nc.vector.tensor_scalar(reserve_v[:], row_stats[:, 1:2], 0.1, reserve_sb[:], ALU.add, ALU.mult)
+        neg_cut = sb.tile([P, 1], F32, name="neg_cut")
+        nc.scalar.activation(neg_cut[:], sd[:], ACT.Identity, bias=negated[:, 0:1], scale=negated[:, 1:2])
+
+        above = [sb.tile([P, HALF], F32, name="above%d" % h) for h in range(2)]
+        part = [sb.tile([P, HALF], F32, name="part%d" % h) for h in range(2)]
+        part_sum = [sb.tile([P, 1], F32, name="part_sum%d" % h) for h in range(2)]
+        nc.vector.tensor_scalar(above[0][:], score[0][:], neg_cut[:], 0.0, ALU.add, ALU.max)
+        nc.scalar.activation(above[1][:], score[1][:], ACT.Relu, bias=neg_cut[:])
+        nc.vector.scalar_tensor_tensor(part[0][:], score[0][:], neg_cut[:], above[0][:], ALU.add, ALU.mult, accum_out=part_sum[0][:])
+        nc.scalar.activation(part[1][:], above[1][:], ACT.Square, accum_out=part_sum[1][:])
+
+        weighted = sb.tile([P, SLOTS], F32, name="weighted")
+        by_run = weighted[:].rearrange("p (g k) -> p g k", k=RUN)
         run_sums = sb.tile([P, G], F32, name="run_sums")
-        nc.vector.tensor_reduce(run_sums[:, 0 : G // 2], weighted[:, 0 : G // 2, :], AXIS.X, ALU.add)
+        denom = sb.tile([P, 1], F32, name="denom")
         inv = sb.tile([P, 1], F32, name="inv")
+        nc.vector.tensor_tensor(weighted[:, HALF:], part[1][:], worth_all[:, HALF:], ALU.mult)
+        nc.vector.scalar_tensor_tensor(denom[:], part_sum[0][:], part_sum[1][:], reserve_v[:], ALU.add, ALU.add)
+        nc.vector.tensor_tensor(weighted[:, :HALF], part[0][:], worth_all[:, :HALF], ALU.mult)
         nc.vector.reciprocal(inv[:], denom[:])
-        nc.vector.tensor_reduce(run_sums[:, G // 2 : G], weighted[:, G // 2 : G, :], AXIS.X, ALU.add)
+        nc.vector.tensor_reduce(run_sums[:, G // 2 : G], by_run[:, G // 2 : G, :], AXIS.X, ALU.add)
+        nc.vector.tensor_reduce(run_sums[:, 0 : G // 2], by_run[:, 0 : G // 2, :], AXIS.X, ALU.add)
         factor = sb.tile([P, G], F32, name="factor")
         nc.scalar.activation(factor[:], const256[:], ACT.Copy, scale=inv[:])
         nc.vector.tensor_tensor(placed[:].indirect(col_list[:]), run_sums[:], factor[:], ALU.mult)

@@ -40,6 +40,7 @@ def tile_attend_relayed_outliers_pagesums_kernel(
         tie_words = sb.tile([P, T], U32, name="tie_words")
         tie_scales = sb.tile([P, T], U8, name="tie_scales")
         worth_sb = sb.tile([P, T], F32, name="worth_sb", tag="worth_then_sd")
+        slot_scales = sb.tile([P, SLOTS], U8, name="slot_scales", align_bytes=64)
         q_raw = sb.tile([P, PACK, Q], F32, name="q_raw")
         old_sb = sb.tile([P, M], F32, name="old_sb")
         placed = sb.tile([P, M], F32, name="placed")
@@ -52,39 +53,37 @@ def tile_attend_relayed_outliers_pagesums_kernel(
         nc.vector.memset(placed[:], 0.0)
         nc.scalar.activation(const256[:], placed[:, 0:G], ACT.Sqrt, bias=65536.0)
 
+        nc.vector.memset(slot_scales[:].bitcast(I32), 0)
+
         hub_planes = hubs.rearrange("(p t) u -> p t u", t=PACK)
+        nc.sync.dma_start(planes[0][:], hub_planes[:, 0, :])
         nc.sync.dma_start(hub_list[:], offs2)
         nc.sync.dma_start(tok_list[:], offs)
-        nc.sync.dma_start(planes[0][:], hub_planes[:, 0, :])
-        for quad in range(4):
-            nc.sync.dma_start(
-                tie_scales[32 * quad : 32 * quad + 4, :].bitcast(I32),
-                ties_scales[0, 4 * quad : 4 * quad + 4, :].bitcast(I32),
-            )
+        nc.sync.dma_start(tie_scales[0:P:8, :].bitcast(I32), ties_scales[0].bitcast(I32))
         for t in range(1, PACK):
             nc.sync.dma_start(planes[t][:], hub_planes[:, t, :])
         nc.sync.dma_start(q_raw[:], query.rearrange("(p t) q -> p t q", t=PACK))
         nc.sync.dma_start(tie_words[:].bitcast(I32), ties_words[0].rearrange("p n t -> p (n t)").bitcast(I32))
-        nc.sync.dma_start(hf_sb[:], hf.rearrange("(p t) o -> p (t o)", t=PACK))
-        nc.sync.dma_start(worth_sb[:], worth)
-        nc.sync.dma_start(row_stats[:, 8:9], bar)
-        nc.sync.dma_start(reserve_sb[:], reserve)
         nc.sync.dma_start(col_list[:], offs3)
-        nc.sync.dma_start(old_sb[:], old)
-
-        lo, hi = slice(0, LIST_COLS // 2), slice(LIST_COLS // 2, LIST_COLS)
+        nc.gpsimd.dma_start(hf_sb[:], hf.rearrange("(p t) o -> p (t o)", t=PACK))
+        nc.gpsimd.dma_start(row_stats[:, 8:9], bar)
+        nc.gpsimd.dma_start(reserve_sb[:], reserve)
 
         hub_bf = sb.tile([P, PACK, P, PACK], BF16, name="hub_bf", align_bytes=64)
         staged = sb.tile([P, PACK, J - J_VECTOR], BF16, name="staged")
-        scale_g = [sb.tile([P, HALF], U8, name="scale_g%d" % h, align_bytes=64) for h in range(2)]
+        scale_g = sb.tile([P, SLOTS], U8, name="scale_g")
         for t in range(PACK):
             nc.scalar.activation(staged[:, t, :], planes[t][:].indirect(hub_list[:, J_VECTOR // 16 :]), ACT.Copy)
             nc.vector.tensor_copy(
                 hub_bf[:, :, 0 : J_VECTOR // PACK, t].rearrange("p r m -> p m r"),
                 planes[t][:].indirect(hub_list[:, 0 : J_VECTOR // 16]),
             )
-            if t in (0, 1):
-                nc.vector.tensor_copy(scale_g[t][:], tie_scales[:].indirect(tok_list[:, (lo, hi)[t]]))
+            if t == 0:
+                nc.vector.tensor_copy(scale_g[:], tie_scales[:].indirect(tok_list[:]))
+        for f in range(4):
+            nc.sync.dma_start(slot_scales[f:P:32, :].bitcast(I32), scale_g[8 * f : P : 32, :].bitcast(I32))
+        nc.sync.dma_start(worth_sb[:], worth)
+        nc.sync.dma_start(old_sb[:], old)
         nc.vector.tensor_copy(
             hub_bf[:, :, J_VECTOR // PACK : P, :].rearrange("p r (a b) t -> p a r b t", b=2),
             staged[:].rearrange("p t (a b r) -> p a r b t", b=2, r=PACK),
@@ -132,10 +131,8 @@ def tile_attend_relayed_outliers_pagesums_kernel(
         hp_codes = sb.tile([P, Q], U32, name="hp_codes", align_bytes=64)
         hp_scales = sb.tile([P, Q], U8, name="hp_scales", align_bytes=64)
 
-        def gather_words(first, count, tag):
-            words = sb.tile([P, count], U32, name=tag + "_words", tag=tag, align_bytes=64)
-            nc.vector.tensor_copy(words[:], tie_words[:].indirect(tok_list[:, first // 16 : (first + count) // 16]))
-            return words
+        def gather_words(words, first, count):
+            nc.vector.tensor_copy(words, tie_words[:].indirect(tok_list[:, first // 16 : (first + count) // 16]))
 
         def score_slots(first, count, words):
             h, cols = first // HALF, slice(first % HALF, first % HALF + count)
@@ -143,19 +140,21 @@ def tile_attend_relayed_outliers_pagesums_kernel(
                 out=score[h][:, cols],
                 lhsT=hp_codes[:].bitcast(FP8X4),
                 lhsT_scale=hp_scales[:],
-                rhs=words[:].bitcast(FP8X4),
-                rhs_scale=scale_g[h][:, cols],
+                rhs=words.bitcast(FP8X4),
+                rhs_scale=slot_scales[:, first : first + count],
                 start=True,
                 stop=True,
             )
 
-        words_a = gather_words(0, HALF, "first_half")
-        words_b = gather_words(HALF, QUARTER, "hf_then_words")
+        early_words = sb.tile([P, QUARTER], U32, name="early_words", tag="hf_then_words", align_bytes=64)
+        gather_words(early_words[:], 0, QUARTER)
         nc.vector.quantize_mx(out=hp_codes[:].bitcast(FP8X4), scales=hp_scales[:], in_=hp_bf[:].rearrange("p q t -> p (q t)"))
-        words_c = gather_words(HALF + QUARTER, QUARTER, "hp_then_words")
-        score_slots(0, HALF, words_a)
-        score_slots(HALF, QUARTER, words_b)
-        score_slots(HALF + QUARTER, QUARTER, words_c)
+        late_words = sb.tile([P, SLOTS - QUARTER], U32, name="late_words", tag="hp_then_words", align_bytes=64)
+        gather_words(late_words[:, :QUARTER], QUARTER, QUARTER)
+        gather_words(late_words[:, QUARTER:], HALF, HALF)
+        score_slots(0, QUARTER, early_words[:])
+        score_slots(QUARTER, QUARTER, late_words[:, :QUARTER])
+        score_slots(HALF, HALF, late_words[:, QUARTER:])
         stats = sb.tile([P, 12], F32, name="stats")
         for h in range(2):
             nc.vector.bn_stats(stats[:, 6 * h : 6 * h + 6], score[h][:])

@@ -131,8 +131,10 @@ def tile_attend_relayed_outliers_pagesums_kernel(
         hp_codes = sb.tile([P, Q], U32, name="hp_codes", align_bytes=64)
         hp_scales = sb.tile([P, Q], U8, name="hp_scales", align_bytes=64)
 
-        def gather_words(words, first, count):
-            nc.vector.tensor_copy(words, tie_words[:].indirect(tok_list[:, first // 16 : (first + count) // 16]))
+        def gather_words(first, count, tag):
+            words = sb.tile([P, count], U32, name=tag + "_words", tag=tag, align_bytes=64)
+            nc.vector.tensor_copy(words[:], tie_words[:].indirect(tok_list[:, first // 16 : (first + count) // 16]))
+            return words
 
         def score_slots(first, count, words):
             h, cols = first // HALF, slice(first % HALF, first % HALF + count)
@@ -140,21 +142,19 @@ def tile_attend_relayed_outliers_pagesums_kernel(
                 out=score[h][:, cols],
                 lhsT=hp_codes[:].bitcast(FP8X4),
                 lhsT_scale=hp_scales[:],
-                rhs=words.bitcast(FP8X4),
+                rhs=words[:].bitcast(FP8X4),
                 rhs_scale=slot_scales[:, first : first + count],
                 start=True,
                 stop=True,
             )
 
-        early_words = sb.tile([P, QUARTER], U32, name="early_words", tag="hf_then_words", align_bytes=64)
-        gather_words(early_words[:], 0, QUARTER)
+        words_a = gather_words(0, HALF, "first_half")
+        words_b = gather_words(HALF, QUARTER, "hf_then_words")
         nc.vector.quantize_mx(out=hp_codes[:].bitcast(FP8X4), scales=hp_scales[:], in_=hp_bf[:].rearrange("p q t -> p (q t)"))
-        late_words = sb.tile([P, SLOTS - QUARTER], U32, name="late_words", tag="hp_then_words", align_bytes=64)
-        gather_words(late_words[:, :QUARTER], QUARTER, QUARTER)
-        gather_words(late_words[:, QUARTER:], HALF, HALF)
-        score_slots(0, QUARTER, early_words[:])
-        score_slots(QUARTER, QUARTER, late_words[:, :QUARTER])
-        score_slots(HALF, HALF, late_words[:, QUARTER:])
+        words_c = gather_words(HALF + QUARTER, QUARTER, "hp_then_words")
+        score_slots(0, HALF, words_a)
+        score_slots(HALF, QUARTER, words_b)
+        score_slots(HALF + QUARTER, QUARTER, words_c)
         stats = sb.tile([P, 12], F32, name="stats")
         for h in range(2):
             nc.vector.bn_stats(stats[:, 6 * h : 6 * h + 6], score[h][:])

from contextlib import ExitStack

import concourse.mybir as mybir

F32 = mybir.dt.float32
BF16 = mybir.dt.bfloat16
I32 = mybir.dt.int32
U32 = mybir.dt.uint32
U16 = mybir.dt.uint16
U8 = mybir.dt.uint8
FP8X4 = mybir.dt.float8_e4m3fn_x4
ALU = mybir.AluOpType
ACT = mybir.ActivationFunctionType
AXIS = mybir.AxisListType

P = 128
PACK = 4
D, T, SLOTS, Q, J, U, G, M = 512, 2048, 512, 128, 512, 1024, 64, 512
RUN = SLOTS // G
HALF = SLOTS // 2
QUARTER = SLOTS // 4
LIST_COLS = SLOTS // 16
J_VECTOR = 224

FLOPS = 2 * D * J * Q + 2 * J * Q * SLOTS


def tile_attend_relayed_outliers_pagesums_kernel(
    tc, query, hubs, hf, ties_words, ties_scales, bar, reserve, worth, old, offs, offs2, offs3, out
):
    nc = tc.nc
    with ExitStack() as ctx:
        sb = ctx.enter_context(tc.tile_pool(name="sb", bufs=1))
        ps = ctx.enter_context(tc.psum_pool(name="ps", bufs=1))

        tok_list = sb.tile([P, LIST_COLS], U16, name="tok_list")
        hub_list = sb.tile([P, LIST_COLS], U16, name="hub_list")
        col_list = sb.tile([P, G // 16], U16, name="col_list")
        planes = [sb.tile([P, U], F32, name="plane%d" % t) for t in range(PACK)]
        tie_words = sb.tile([P, T], U32, name="tie_words")
        tie_scales = sb.tile([P, T], U8, name="tie_scales")
        worth_sb = sb.tile([P, T], F32, name="worth_sb", tag="worth_then_sd")
        slot_scales = sb.tile([P, SLOTS], U8, name="slot_scales", align_bytes=64)
        q_raw = sb.tile([P, PACK, Q], F32, name="q_raw")
        old_sb = sb.tile([P, M], F32, name="old_sb")
        placed = sb.tile([P, M], F32, name="placed")
        hf_sb = sb.tile([P, PACK], F32, name="hf_sb", tag="hf_then_words", align_bytes=64)
        row_stats = sb.tile([P, 16], F32, name="row_stats")
        reserve_sb = sb.tile([P, 1], F32, name="reserve_sb")
        const256 = sb.tile([P, G], F32, name="const256")

        nc.vector.memset(tie_scales[:].bitcast(I32), 0)
        nc.vector.memset(placed[:], 0.0)
        nc.scalar.activation(const256[:], placed[:, 0:G], ACT.Sqrt, bias=65536.0)

        nc.vector.memset(slot_scales[:].bitcast(I32), 0)

        hub_planes = hubs.rearrange("(p t) u -> p t u", t=PACK)
        nc.sync.dma_start(planes[0][:], hub_planes[:, 0, :])
        nc.sync.dma_start(hub_list[:], offs2)
        nc.sync.dma_start(tok_list[:], offs)
        nc.sync.dma_start(tie_scales[0:P:8, :].bitcast(I32), ties_scales[0].bitcast(I32))
        for t in range(1, PACK):
            nc.sync.dma_start(planes[t][:], hub_planes[:, t, :])
        nc.sync.dma_start(q_raw[:], query.rearrange("(p t) q -> p t q", t=PACK))
        nc.sync.dma_start(tie_words[:].bitcast(I32), ties_words[0].rearrange("p n t -> p (n t)").bitcast(I32))
        nc.sync.dma_start(col_list[:], offs3)
        nc.gpsimd.dma_start(hf_sb[:], hf.rearrange("(p t) o -> p (t o)", t=PACK))
        nc.gpsimd.dma_start(row_stats[:, 8:9], bar)
        nc.gpsimd.dma_start(reserve_sb[:], reserve)

        hub_bf = sb.tile([P, PACK, P, PACK], BF16, name="hub_bf", align_bytes=64)
        staged = sb.tile([P, PACK, J - J_VECTOR], BF16, name="staged")
        scale_g = sb.tile([P, SLOTS], U8, name="scale_g")
        for t in range(PACK):
            nc.scalar.activation(staged[:, t, :], planes[t][:].indirect(hub_list[:, J_VECTOR // 16 :]), ACT.Copy)
            nc.vector.tensor_copy(
                hub_bf[:, :, 0 : J_VECTOR // PACK, t].rearrange("p r m -> p m r"),
                planes[t][:].indirect(hub_list[:, 0 : J_VECTOR // 16]),
            )
            if t == 0:
                nc.vector.tensor_copy(scale_g[:], tie_scales[:].indirect(tok_list[:]))
        for f in range(4):
            nc.sync.dma_start(slot_scales[f:P:32, :].bitcast(I32), scale_g[8 * f : P : 32, :].bitcast(I32))
        nc.sync.dma_start(worth_sb[:], worth)
        nc.sync.dma_start(old_sb[:], old)
        nc.vector.tensor_copy(
            hub_bf[:, :, J_VECTOR // PACK : P, :].rearrange("p r (a b) t -> p a r b t", b=2),
            staged[:].rearrange("p t (a b r) -> p a r b t", b=2, r=PACK),
        )

        q_bf = sb.tile([P, Q, PACK], BF16, name="q_bf", align_bytes=64)
        nc.scalar.copy(q_bf[:], q_raw[:].rearrange("p t q -> p q t"))

        worth_all = sb.tile([P, SLOTS], F32, name="worth_all")
        nc.scalar.activation(worth_all[:], worth_sb[:].indirect(tok_list[:]), ACT.Copy)

        hub_codes = sb.tile([P, J], U32, name="hub_codes", align_bytes=64)
        hub_scales = sb.tile([P, J], U8, name="hub_scales", align_bytes=64)
        q_codes = sb.tile([P, Q], U32, name="q_codes", align_bytes=64)
        q_scales = sb.tile([P, Q], U8, name="q_scales", align_bytes=64)
        hb = ps.tile([P, PACK, Q], F32, name="hb")
        nc.vector.quantize_mx(out=q_codes[:].bitcast(FP8X4), scales=q_scales[:], in_=q_bf[:].rearrange("p q t -> p (q t)"))
        for r in range(PACK):
            cols = slice(r * P, (r + 1) * P)
            nc.vector.quantize_mx(
                out=hub_codes[:, cols].bitcast(FP8X4),
                scales=hub_scales[:, cols],
                in_=hub_bf[:, r, :, :].rearrange("p m t -> p (m t)"),
            )
            nc.tensor.matmul_mx(
                out=hb[:, r, :],
                lhsT=hub_codes[:, cols].bitcast(FP8X4),
                lhsT_scale=hub_scales[:, cols],
                rhs=q_codes[:].bitcast(FP8X4),
                rhs_scale=q_scales[:],
                start=True,
                stop=True,
            )

        hp_bf = sb.tile([P, Q, PACK], BF16, name="hp_bf", tag="hp_then_words", align_bytes=64)
        nc.vector.scalar_tensor_tensor(
            hp_bf[:],
            hb[:].rearrange("p r q -> p q r"),
            0.0,
            hf_sb[:].unsqueeze(1).to_broadcast([P, Q, PACK]),
            ALU.max,
            ALU.mult,
        )
        score = [ps.tile([P, HALF], F32, name="score%d" % h) for h in range(2)]
        hp_codes = sb.tile([P, Q], U32, name="hp_codes", align_bytes=64)
        hp_scales = sb.tile([P, Q], U8, name="hp_scales", align_bytes=64)

        def gather_words(first, count, tag):
            words = sb.tile([P, count], U32, name=tag + "_words", tag=tag, align_bytes=64)
            nc.vector.tensor_copy(words[:], tie_words[:].indirect(tok_list[:, first // 16 : (first + count) // 16]))
            return words

        def score_slots(first, count, words):
            h, cols = first // HALF, slice(first % HALF, first % HALF + count)
            nc.tensor.matmul_mx(
                out=score[h][:, cols],
                lhsT=hp_codes[:].bitcast(FP8X4),
                lhsT_scale=hp_scales[:],
                rhs=words[:].bitcast(FP8X4),
                rhs_scale=slot_scales[:, first : first + count],
                start=True,
                stop=True,
            )

        words_a = gather_words(0, HALF, "first_half")
        words_b = gather_words(HALF, QUARTER, "hf_then_words")
        nc.vector.quantize_mx(out=hp_codes[:].bitcast(FP8X4), scales=hp_scales[:], in_=hp_bf[:].rearrange("p q t -> p (q t)"))
        words_c = gather_words(HALF + QUARTER, QUARTER, "hp_then_words")
        score_slots(0, HALF, words_a)
        score_slots(HALF, QUARTER, words_b)
        score_slots(HALF + QUARTER, QUARTER, words_c)
        stats = sb.tile([P, 12], F32, name="stats")
        for h in range(2):
            nc.vector.bn_stats(stats[:, 6 * h : 6 * h + 6], score[h][:])
        nc.vector.bn_aggr(row_stats[:, 0:2], stats[:])
        sd = sb.tile([P, 1], F32, name="sd", tag="worth_then_sd")
        nc.scalar.activation(sd[:], row_stats[:, 1:2], ACT.Sqrt, bias=0.1)
        negated = sb.tile([P, 2], F32, name="negated")
        nc.vector.tensor_scalar(negated[:], row_stats[:, 0:9:8], -1.0, None, ALU.mult)
        reserve_v = sb.tile([P, 1], F32, name="reserve_v")
        nc.vector.tensor_scalar(reserve_v[:], row_stats[:, 1:2], 0.1, reserve_sb[:], ALU.add, ALU.mult)
        neg_cut = sb.tile([P, 1], F32, name="neg_cut")
        nc.scalar.activation(neg_cut[:], sd[:], ACT.Identity, bias=negated[:, 0:1], scale=negated[:, 1:2])

        above = [sb.tile([P, HALF], F32, name="above%d" % h) for h in range(2)]
        part = [sb.tile([P, HALF], F32, name="part%d" % h) for h in range(2)]
        part_sum = [sb.tile([P, 1], F32, name="part_sum%d" % h) for h in range(2)]
        nc.vector.tensor_scalar(above[0][:], score[0][:], neg_cut[:], 0.0, ALU.add, ALU.max)
        nc.scalar.activation(above[1][:], score[1][:], ACT.Relu, bias=neg_cut[:])
        nc.vector.scalar_tensor_tensor(part[0][:], score[0][:], neg_cut[:], above[0][:], ALU.add, ALU.mult, accum_out=part_sum[0][:])
        nc.scalar.activation(part[1][:], above[1][:], ACT.Square, accum_out=part_sum[1][:])

        weighted = sb.tile([P, SLOTS], F32, name="weighted")
        by_run = weighted[:].rearrange("p (g k) -> p g k", k=RUN)
        run_sums = sb.tile([P, G], F32, name="run_sums")
        denom = sb.tile([P, 1], F32, name="denom")
        inv = sb.tile([P, 1], F32, name="inv")
        nc.vector.tensor_tensor(weighted[:, HALF:], part[1][:], worth_all[:, HALF:], ALU.mult)
        nc.vector.scalar_tensor_tensor(denom[:], part_sum[0][:], part_sum[1][:], reserve_v[:], ALU.add, ALU.add)
        nc.vector.tensor_tensor(weighted[:, :HALF], part[0][:], worth_all[:, :HALF], ALU.mult)
        nc.vector.reciprocal(inv[:], denom[:])
        nc.vector.tensor_reduce(run_sums[:, G // 2 : G], by_run[:, G // 2 : G, :], AXIS.X, ALU.add)
        nc.vector.tensor_reduce(run_sums[:, 0 : G // 2], by_run[:, 0 : G // 2, :], AXIS.X, ALU.add)
        factor = sb.tile([P, G], F32, name="factor")
        nc.scalar.activation(factor[:], const256[:], ACT.Copy, scale=inv[:])
        nc.vector.tensor_tensor(placed[:].indirect(col_list[:]), run_sums[:], factor[:], ALU.mult)
        for h, queue in enumerate((nc.sync, nc.scalar)):
            cols = slice(h * (M // 2), (h + 1) * (M // 2))
            result = sb.tile([P, M // 2], F32, name="result%d" % h)
            nc.vector.tensor_tensor(result[:], placed[:, cols], old_sb[:, cols], ALU.add)
            queue.dma_start(out[:, cols], result[:])
